import numpy as np
import ml_dtypes


def mxq(x, axis, fmt="e4m3"):
    dtype, down = {"e4m3": (ml_dtypes.float8_e4m3fn, 7), "e5m2": (ml_dtypes.float8_e5m2, 14)}[fmt]
    v = np.moveaxis(np.asarray(x, np.float32).astype(ml_dtypes.bfloat16).astype(np.float64), axis, -1)
    blocks = v.reshape(v.shape[:-1] + (-1, 32))
    amax = np.abs(blocks).max(-1, keepdims=True)
    byte = np.maximum(np.where(amax > 0, np.frexp(amax)[1] - 1 + 127, 0) - down, 1)
    scale = np.exp2(byte - 127.0)
    codes = (blocks / scale).astype(np.float32).astype(dtype).astype(np.float64)
    return np.moveaxis((codes * scale).reshape(v.shape), -1, axis)


WIDE = False


def mx_kscale(k):
    if not WIDE:
        return np.ones(k)
    levels = np.array([10, -10, 5, -5, 0])
    if k % 512:
        return np.exp2(np.random.permutation(np.resize(levels, k // 32))).repeat(32)
    a = np.empty((k // 512, 16))
    for p in range(k // 512):
        a[p, :8] = np.random.permutation(np.resize(levels, 8))
        for g in range(8):
            far = levels[np.abs(levels - a[p, g]) >= 10]
            a[p, g + 8] = far[np.random.randint(len(far))]
    return np.exp2(a.ravel()).repeat(32)


BF16 = ml_dtypes.bfloat16


def bf(x):
    return np.asarray(x, np.float32).astype(BF16)


def f64(x):
    return np.asarray(x).astype(np.float64)


T, N, M, R, C = 1024, 1024, 1024, 1024, 8
H = M // C
FLOOR = 0.1


def bcpnn_weights(u, v, p, q):
    cov = (mxq(f64(u).T, 1, "e4m3") @ mxq(f64(v), 0, "e4m3")) / u.shape[0]
    ratio = 1.0 + cov / (f64(p)[:, None] * f64(q)[None, :])
    return np.log(np.maximum(ratio, FLOOR))


def softmax(z):
    e = np.exp(z - np.max(z, axis=-1, keepdims=True))
    return e / np.sum(e, axis=-1, keepdims=True)


def draw0():
    s, t = mx_kscale(T), mx_kscale(N)
    a = 0.124 * T**0.25
    return {
        "u": bf(np.random.standard_normal((T, N)) * a * s[:, None]),
        "v": bf(np.random.standard_normal((T, M)) * a / s[:, None]),
        "p": bf(np.random.uniform(0.15, 0.35, N)),
        "q": bf(np.random.uniform(0.15, 0.35, M)),
        "g": bf((1.0 + 0.1 * np.random.standard_normal(N)) * t),
        "x": bf(np.random.standard_normal((R, N)) * 3.2 / np.sqrt(N) / t),
    }


def core(u, v, p, q, g, x):
    w = bcpnn_weights(u, v, p, q)
    wg = f64(g)[:, None] * w
    z = (mxq(f64(x), 1, "e4m3") @ mxq(wg, 0, "e4m3")) + np.log(f64(q))[None, :]
    z = np.reshape(z, (x.shape[0], H, C))
    return softmax(z)


def e4m3fn_bytes(y):
    return np.clip(np.asarray(y, np.float64), -448.0, 448.0).astype(np.float32).astype(ml_dtypes.float8_e4m3fn).view(np.uint8)


def e4m3fn_values(b):
    return np.asarray(b, np.uint8).view(ml_dtypes.float8_e4m3fn).astype(np.float64)


def setup_inputs():
    d = draw0()
    x0 = np.asarray(d['x']).astype(np.float64)
    s = (np.max(np.abs(x0), axis=(0,), keepdims=True) / 448.0).astype(np.float32)
    out = {}
    for k, v in d.items():
        if k == 'x':
            out['x_bytes'] = e4m3fn_bytes(x0 / s.astype(np.float64))
            out['x_scale'] = s
        else:
            out[k] = v
    return out


def reference(u, v, p, q, g, x_bytes, x_scale):
    return core(u, v, p, q, g, e4m3fn_values(x_bytes) * x_scale.astype(np.float64))

@@ -1,0 +1,518 @@
+from contextlib import ExitStack
+
+import concourse.mybir as mybir
+from concourse.masks import make_identity
+
+T, N, M, R, C = 1024, 1024, 1024, 1024, 8
+H = M // C
+FLOOR = 0.1
+FLOPS = 2 * T * N * M + 2 * R * N * M
+
+F32 = mybir.dt.float32
+BF16 = mybir.dt.bfloat16
+U32 = mybir.dt.uint32
+U8 = mybir.dt.uint8
+FP8 = mybir.dt.float8_e4m3fn
+FP8X4 = mybir.dt.float8_e4m3fn_x4
+ALU = mybir.AluOpType
+ACT = mybir.ActivationFunctionType
+AXIS = mybir.AxisListType
+
+P = 128
+PACK = 4
+KP = P * PACK
+BANK = 512
+HALF = 512
+BLOCKS = R // P
+
+
+def tile_bcpnnhypercolumnrecall_kernel(tc, u, v, p, q, g, x_bytes, x_scale, out):
+    nc = tc.nc
+    with ExitStack() as ctx:
+        keep = ctx.enter_context(tc.tile_pool(name="keep", bufs=1))
+        work = ctx.enter_context(tc.tile_pool(name="work", bufs=2))
+        psum = ctx.enter_context(tc.psum_pool(name="psum", bufs=1))
+        ctx.enter_context(tc.manual_schedule())
+
+        banks_taken = []
+
+        def next_bank(shape, dtype=F32):
+            tag = "bank_%d" % (len(banks_taken) % 7)
+            banks_taken.append(tag)
+            return psum.tile(list(shape), dtype, name=tag, tag=tag)
+
+        def small_bank(shape):
+            return psum.tile(list(shape), F32, name="small", tag="small", bufs=1)
+
+        def mx_tiles(name, width):
+            codes = keep.tile([P, width], U32, name=name + "_codes", align_bytes=64)
+            scales = keep.tile([P, width], U8, name=name + "_scales", align_bytes=64)
+            return codes, scales
+
+        def quantize(dst, src):
+            nc.vector.quantize_mx(out=dst[0][:].bitcast(FP8X4), scales=dst[1][:], in_=src)
+
+        def load_rows(name, src, kh, half):
+            raw = work.tile([P, PACK, HALF], BF16, name="raw", tag="wide", bufs=8)
+            rows = src[kh * KP : (kh + 1) * KP, half * HALF : (half + 1) * HALF]
+            nc.sync.dma_start(out=raw[:], in_=rows.rearrange("(p j) n -> p j n", j=PACK))
+            return raw
+
+        def load_x(first, count):
+            xb = keep.tile([P, count, N], U8, name="x_bytes_%d" % first)
+            rows = x_bytes[first * P : (first + count) * P, :]
+            nc.sync.dma_start(out=xb[:], in_=rows.rearrange("(b p) k -> p b k", p=P))
+            return [xb[:, b, :] for b in range(count)]
+
+        q_sb = keep.tile([P, C], BF16, name="q_sb")
+        p_sb = keep.tile([P, 2, PACK], BF16, name="p_sb")
+        g_sb = keep.tile([P, 2, PACK], BF16, name="g_sb")
+        x_scales = keep.tile([P, N], F32, name="x_scales")
+        u_raw = {}
+        v_raw = {}
+        s_sb = keep.tile([P, C], F32, name="s_sb")
+        nc.sync.dma_start(out=s_sb[:], in_=x_scale.rearrange("o (a b) -> (o a) b", b=C))
+        nc.sync.dma_start(out=q_sb[:], in_=q.rearrange("(h c) -> h c", c=C))
+        x_rows = load_x(0, 2)
+        u_raw[0, 0] = load_rows("u", u, 0, 0)
+        u_raw[1, 0] = load_rows("u", u, 1, 0)
+        v_raw[0, 0] = load_rows("v", v, 0, 0)
+        v_raw[1, 0] = load_rows("v", v, 1, 0)
+        nc.sync.dma_start(out=p_sb[:], in_=p.rearrange("(a p t) -> p a t", p=P, t=PACK))
+        nc.sync.dma_start(out=g_sb[:], in_=g.rearrange("(a p t) -> p a t", p=P, t=PACK))
+        v_raw[0, 1] = load_rows("v", v, 0, 1)
+        v_raw[1, 1] = load_rows("v", v, 1, 1)
+        u_raw[0, 1] = load_rows("u", u, 0, 1)
+        u_raw[1, 1] = load_rows("u", u, 1, 1)
+        x_rows = x_rows + load_x(2, BLOCKS - 2)
+
+        ident = keep.tile([P, P], F32, name="ident")
+        ident_bf = keep.tile([P, P], BF16, name="ident_bf")
+        make_identity(nc, ident[:])
+        nc.vector.tensor_copy(out=ident_bf[:], in_=ident[:])
+        log_q = keep.tile([P, C], F32, name="log_q")
+        inv_q = keep.tile([P, C], F32, name="inv_q")
+        nc.scalar.activation(out=log_q[:], in_=q_sb[:], func=ACT.Ln)
+        nc.vector.reciprocal(out=inv_q[:], in_=q_sb[:])
+        inv_q_rows = keep.tile([P, C, H], F32, name="inv_q_rows")
+        inv_p = keep.tile([P, 2, PACK], F32, name="inv_p")
+        row_factor = keep.tile([P, 2, PACK], F32, name="row_factor")
+        gain = keep.tile([P, 2, PACK], F32, name="gain")
+
+        def spread_inv_q():
+            for ch in range(2):
+                bank = next_bank((P, 4, H))
+                for c in range(4):
+                    column = inv_q[:, 4 * ch + c : 4 * ch + c + 1].to_broadcast([P, P])
+                    nc.tensor.transpose(bank[:, c, :], column, ident[:])
+                nc.scalar.copy(out=inv_q_rows[:, 4 * ch : 4 * ch + 4, :], in_=bank[:])
+
+        def spread_x_scale():
+            for ch in range(2):
+                bank = next_bank((P, 4, P))
+                for b in range(4):
+                    column = s_sb[:, 4 * ch + b : 4 * ch + b + 1].to_broadcast([P, P])
+                    nc.tensor.transpose(bank[:, b, :], column, ident[:])
+                nc.scalar.copy(
+                    out=x_scales[:].rearrange("p (a b) -> p a b", b=C)[:, :, 4 * ch : 4 * ch + 4],
+                    in_=bank[:].rearrange("p b a -> p a b"),
+                )
+
+        def row_constants():
+            nc.vector.reciprocal(out=inv_p[:], in_=p_sb[:])
+            nc.vector.tensor_copy(out=gain[:], in_=g_sb[:])
+            nc.vector.tensor_scalar(out=row_factor[:], in0=inv_p[:], scalar1=1.0 / T, scalar2=None, op0=ALU.mult)
+
+        u_mx = {}
+        v_mx = {}
+        grouped = {}
+        grouping = {}
+
+        def group_on_tensor(key, raw, columns):
+            for pair in range(2):
+                bank = next_bank((P, 2, BANK), BF16)
+                for s in range(2):
+                    moving = raw[:, :, columns(2 * pair + s)].rearrange("p j n -> p n j")
+                    nc.tensor.matmul(out=bank[:, s, :], lhsT=ident_bf[:], rhs=moving, start=True, stop=True)
+                grouping[key, pair] = bank
+
+        def collect(*key):
+            tile = work.tile([P, HALF * PACK], BF16, name="grouped", tag="grouped", bufs=4, align_bytes=64)
+            for pair in range(2):
+                nc.scalar.copy(
+                    out=tile[:, pair * 2 * BANK : (pair + 1) * 2 * BANK],
+                    in_=grouping[key, pair][:].rearrange("p s n -> p (s n)"),
+                )
+            grouped[key] = tile
+
+        def group_on_vector(key, raw):
+            tile = work.tile([P, HALF * PACK], BF16, name="grouped", tag="grouped", bufs=4, align_bytes=64)
+            nc.vector.tensor_copy(
+                out=tile[:].rearrange("p (n i j) -> p n j i", i=4, j=PACK),
+                in_=raw[:].rearrange("p j (n i) -> p n j i", i=4),
+            )
+            grouped[key] = tile
+
+        def group_u(kh, ih):
+            group_on_tensor(("u", kh, ih), u_raw[kh, ih], lambda t: slice(t, HALF, PACK))
+
+        def group_v_on_tensor(kh, jh):
+            group_on_tensor(("v", kh, jh), v_raw[kh, jh], lambda s: slice(s * P, (s + 1) * P))
+
+        def quantize_u(kh, ih):
+            u_mx[kh, ih] = mx_tiles("u_%d_%d" % (kh, ih), HALF)
+            quantize(u_mx[kh, ih], grouped["u", kh, ih][:])
+
+        def quantize_v(kh, jh):
+            v_mx[kh, jh] = mx_tiles("v_%d_%d" % (kh, jh), HALF)
+            quantize(v_mx[kh, jh], grouped["v", kh, jh][:])
+
+        cov = {}
+        ratio = {}
+        planes = {}
+        w_grouped = {}
+        w_mx = {}
+
+        def covariance(ih, jh, t):
+            bank = next_bank((P, BANK))
+            cols = slice(t * P, (t + 1) * P)
+            for kh in range(2):
+                nc.tensor.matmul_mx(
+                    out=bank[:],
+                    lhsT=u_mx[kh, ih][0][:, cols].bitcast(FP8X4),
+                    lhsT_scale=u_mx[kh, ih][1][:, cols],
+                    rhs=v_mx[kh, jh][0][:].bitcast(FP8X4),
+                    rhs_scale=v_mx[kh, jh][1][:],
+                    start=(kh == 0),
+                    stop=(kh == 1),
+                )
+            cov[ih, jh, t] = bank
+
+        def normalise(ih, jh, t):
+            if t == 0:
+                ratio[ih, jh] = work.tile([P, PACK, HALF], F32, name="ratio", tag="ratio", bufs=3)
+            nc.vector.scalar_tensor_tensor(
+                out=ratio[ih, jh][:, t, :].rearrange("p (c h) -> p c h", c=C),
+                in0=cov[ih, jh, t][:].rearrange("p (h c) -> p c h", c=C),
+                scalar=row_factor[:, ih, t : t + 1],
+                in1=inv_q_rows[:, :, jh * (H // 2) : (jh + 1) * (H // 2)],
+                op0=ALU.mult,
+                op1=ALU.mult,
+            )
+
+        def clamp(ih, jh, first, count):
+            part = ratio[ih, jh][:, first : first + count, :]
+            nc.scalar.activation(out=part, in_=part, func=ACT.Relu, bias=1.0 - FLOOR)
+
+        def logarithm(ih, jh, first, count):
+            part = ratio[ih, jh][:, first : first + count, :]
+            nc.scalar.activation(out=part, in_=part, func=ACT.Ln, bias=FLOOR)
+
+        def apply_gain(ih, jh, t, on_scalar):
+            if (ih, jh) not in planes:
+                planes[ih, jh] = work.tile([P, PACK, HALF], BF16, name="planes", tag="planes", bufs=2)
+            factor = gain[:, ih, t : t + 1]
+            if on_scalar:
+                nc.scalar.activation(out=planes[ih, jh][:, t, :], in_=ratio[ih, jh][:, t, :], func=ACT.Copy, scale=factor)
+            else:
+                nc.vector.tensor_scalar(
+                    out=planes[ih, jh][:, t, :], in0=ratio[ih, jh][:, t, :], scalar1=factor, scalar2=None, op0=ALU.mult
+                )
+
+        def group_w(ih, jh, ch):
+            if jh == 0:
+                w_grouped[ih, ch] = work.tile([P, 4, H, PACK], BF16, name="w_grouped", tag="w_grouped", bufs=4, align_bytes=64)
+            dst = w_grouped[ih, ch][:, :, jh * (H // 2) : (jh + 1) * (H // 2), :]
+            src = planes[ih, jh][:, :, ch * (HALF // 2) : (ch + 1) * (HALF // 2)]
+            nc.vector.tensor_copy(
+                out=dst.rearrange("p c (n i) t -> p c n t i", i=4),
+                in_=src.rearrange("p t (c n i) -> p c n t i", c=4, i=4),
+            )
+
+        def quantize_w(ih, ch):
+            w_mx[ih, ch] = mx_tiles("w_%d_%d" % (ih, ch), 4 * H)
+            quantize(w_mx[ih, ch], w_grouped[ih, ch][:].rearrange("p c h t -> p (c h t)"))
+
+        x_value = {}
+        x_turned = {}
+        x_grouped = {}
+        x_mx = {}
+
+        def scale_x(b):
+            x_value[b] = work.tile([P, N], BF16, name="x_value", tag="x_value", bufs=8)
+            nc.vector.tensor_tensor(out=x_value[b][:], in0=x_rows[b].bitcast(FP8), in1=x_scales[:], op=ALU.mult)
+
+        def turn_x(b):
+            words = x_value[b][:].bitcast(F32)
+            bank = next_bank((P, 2, 2, P))
+            for ih in range(2):
+                for w in range(2):
+                    nc.tensor.transpose(bank[:, ih, w, :], words[:, 256 * ih + w : 256 * (ih + 1) : 2], ident[:])
+            x_turned[b] = bank
+
+        def collect_x(b):
+            bank = x_turned[b]
+            x_grouped[b] = work.tile([P, N], BF16, name="x_grouped", tag="x_grouped", bufs=6, align_bytes=64)
+            nc.scalar.copy(
+                out=x_grouped[b][:].bitcast(F32).rearrange("p (a r w) -> p a r w", a=2, w=2),
+                in_=bank[:].rearrange("p a w r -> p a r w"),
+            )
+
+        def quantize_x(b):
+            x_mx[b] = mx_tiles("x_%d" % b, 2 * P)
+            quantize(x_mx[b], x_grouped[b][:])
+
+        z = {}
+        top = {}
+        shifted = {}
+        expd = {}
+        turned = {}
+        sums = {}
+        inv_sum = {}
+        result = {}
+
+        def support(b, ch):
+            if True:
+                bank = next_bank((P, 4, P))
+                for c in range(4):
+                    cols = slice(c * H, (c + 1) * H)
+                    for ih in range(2):
+                        rows = slice(ih * P, (ih + 1) * P)
+                        nc.tensor.matmul_mx(
+                            out=bank[:, c, :],
+                            lhsT=w_mx[ih, ch][0][:, cols].bitcast(FP8X4),
+                            lhsT_scale=w_mx[ih, ch][1][:, cols],
+                            rhs=x_mx[b][0][:, rows].bitcast(FP8X4),
+                            rhs_scale=x_mx[b][1][:, rows],
+                            start=(ih == 0),
+                            stop=(ih == 1),
+                        )
+                z[b, ch] = bank
+
+        def half_max(b, ch):
+            if ch == 0:
+                top[b] = work.tile([P, 3, P], F32, name="top", tag="top", bufs=3)
+            nc.vector.tensor_reduce(out=top[b][:, ch, :], in_=z[b, ch][:].rearrange("p c r -> p r c"), axis=AXIS.X, op=ALU.max)
+
+        def full_max(b):
+            nc.vector.tensor_tensor(out=top[b][:, 2, :], in0=top[b][:, 0, :], in1=top[b][:, 1, :], op=ALU.max)
+
+        def shift(b, ch):
+            if ch == 0:
+                shifted[b] = work.tile([P, C, P], F32, name="shifted", tag="shifted", bufs=3)
+            nc.vector.tensor_tensor(
+                out=shifted[b][:, 4 * ch : 4 * ch + 4, :],
+                in0=z[b, ch][:],
+                in1=top[b][:, 2:3, :].broadcast_to([P, 4, P]),
+                op=ALU.subtract,
+            )
+
+        def exponentiate(b, ch):
+            if ch == 0:
+                expd[b] = work.tile([P, C, P], F32, name="expd", tag="wide", bufs=8)
+            for c in range(4 * ch, 4 * ch + 4):
+                nc.scalar.activation(out=expd[b][:, c, :], in_=shifted[b][:, c, :], func=ACT.Exp, bias=log_q[:, c : c + 1])
+
+        def add_up(b, batch):
+            if b == batch[0]:
+                sums[batch] = small_bank((P, len(batch), H)) if len(batch) > 1 else next_bank((P, 1, H))
+            for c in range(C):
+                nc.tensor.matmul(
+                    out=sums[batch][:, b - batch[0], :],
+                    lhsT=expd[b][:, c, :],
+                    rhs=ident[:],
+                    start=(c == 0),
+                    stop=(c == C - 1),
+                    is_transpose=True,
+                )
+
+        def turn_back(b, ch):
+            bank = next_bank((P, 4, H))
+            for c in range(4):
+                nc.tensor.transpose(bank[:, c, :], expd[b][:, 4 * ch + c, :], ident[:])
+            turned[b, ch] = bank
+
+        def invert(batch, on_scalar):
+            inverse = keep.tile([P, len(batch), H], F32, name="inv_sum_%d" % batch[0])
+            if on_scalar:
+                nc.scalar.activation(out=inverse[:], in_=sums[batch][:], func=ACT.Ln)
+                nc.scalar.activation(out=inverse[:], in_=inverse[:], func=ACT.Exp, scale=-1.0)
+            else:
+                nc.vector.reciprocal(out=inverse[:], in_=sums[batch][:])
+            for b in batch:
+                inv_sum[b] = inverse[:, b - batch[0], :]
+
+        def divide(b, ch):
+            if ch == 0:
+                result[b] = work.tile([P, H, C], F32, name="result", tag="result", bufs=4)
+            nc.vector.tensor_tensor(
+                out=result[b][:, :, 4 * ch : 4 * ch + 4],
+                in0=turned[b, ch][:].rearrange("p c h -> p h c"),
+                in1=inv_sum[b].unsqueeze(2).broadcast_to([P, H, 4]),
+                op=ALU.mult,
+            )
+
+        def store(b):
+            nc.sync.dma_start(
+                out=out[b * P : (b + 1) * P].rearrange("r h c -> r (h c)"), in_=result[b][:].rearrange("p h c -> p (h c)")
+            )
+
+        units = [(0, 0), (0, 1), (1, 0), (1, 1)]
+
+        def covariances(k):
+            for t in range(PACK):
+                covariance(*units[k], t)
+
+        def gains(k, ts, on_scalar):
+            for t in ts:
+                apply_gain(*units[k], t, on_scalar)
+
+        spread_x_scale()
+        group_u(0, 0)
+        collect("u", 0, 0)
+        scale_x(0)
+        scale_x(1)
+        group_u(1, 0)
+        collect("u", 1, 0)
+        spread_inv_q()
+        group_on_vector(("v", 0, 0), v_raw[0, 0])
+        quantize_u(0, 0)
+        quantize_v(0, 0)
+        group_on_vector(("v", 1, 0), v_raw[1, 0])
+        quantize_u(1, 0)
+        row_constants()
+        quantize_v(1, 0)
+        group_v_on_tensor(0, 1)
+        collect("v", 0, 1)
+        covariances(0)
+        quantize_v(0, 1)
+        normalise(0, 0, 0)
+        normalise(0, 0, 1)
+        clamp(0, 0, 0, 2)
+        group_v_on_tensor(1, 1)
+        normalise(0, 0, 2)
+        normalise(0, 0, 3)
+        group_u(0, 1)
+        clamp(0, 0, 2, 2)
+        collect("v", 1, 1)
+        logarithm(0, 0, 0, 2)
+        scale_x(2)
+        quantize_v(1, 1)
+        covariances(1)
+        scale_x(3)
+        logarithm(0, 0, 2, 2)
+        collect("u", 0, 1)
+        group_u(1, 1)
+        normalise(0, 1, 0)
+        normalise(0, 1, 1)
+        clamp(0, 1, 0, 2)
+        normalise(0, 1, 2)
+        normalise(0, 1, 3)
+        collect("u", 1, 1)
+        clamp(0, 1, 2, 2)
+        gains(0, (0, 1, 2, 3), False)
+        quantize_u(0, 1)
+        logarithm(0, 1, 0, 2)
+        logarithm(0, 1, 2, 2)
+        group_w(0, 0, 0)
+        quantize_u(1, 1)
+        covariances(2)
+        group_w(0, 0, 1)
+        normalise(1, 0, 0)
+        normalise(1, 0, 1)
+        clamp(1, 0, 0, 2)
+        normalise(1, 0, 2)
+        normalise(1, 0, 3)
+        clamp(1, 0, 2, 2)
+        covariances(3)
+        gains(1, (0, 1, 2, 3), False)
+        logarithm(1, 0, 0, 2)
+        logarithm(1, 0, 2, 2)
+        normalise(1, 1, 0)
+        normalise(1, 1, 1)
+        clamp(1, 1, 0, 2)
+        normalise(1, 1, 2)
+        normalise(1, 1, 3)
+        turn_x(0)
+        turn_x(1)
+        clamp(1, 1, 2, 2)
+        group_w(0, 1, 0)
+        group_w(0, 1, 1)
+        logarithm(1, 1, 0, 2)
+        logarithm(1, 1, 2, 2)
+        gains(2, (0, 1), False)
+        gains(2, (2, 3), True)
+        gains(3, (0, 1, 2, 3), True)
+        quantize_w(0, 0)
+        quantize_w(0, 1)
+        scale_x(4)
+        scale_x(5)
+        group_w(1, 0, 0)
+        group_w(1, 0, 1)
+        collect_x(0)
+        collect_x(1)
+        turn_x(2)
+        turn_x(3)
+        turn_x(4)
+        turn_x(5)
+        scale_x(6)
+        group_w(1, 1, 0)
+        group_w(1, 1, 1)
+        quantize_x(0)
+        quantize_w(1, 0)
+        quantize_w(1, 1)
+        support(0, 0)
+        support(0, 1)
+        for b in range(2, 6):
+            collect_x(b)
+        turn_x(6)
+        quantize_x(1)
+        scale_x(7)
+        support(1, 0)
+        support(1, 1)
+        collect_x(6)
+        turn_x(7)
+        collect_x(7)
+        quantize_x(2)
+
+        batches = [(0, 1, 2), (3, 4, 5, 6), (7,)]
+        batch_of = {b: batch for batch in batches for b in batch}
+
+        half_max(0, 0)
+        half_max(0, 1)
+        support(2, 0)
+        quantize_x(3)
+        full_max(0)
+        for b in range(BLOCKS):
+            for ch in range(2):
+                if b + 1 < BLOCKS:
+                    half_max(b + 1, ch)
+                shift(b, ch)
+                exponentiate(b, ch)
+                if 2 * b + ch + 5 < 2 * BLOCKS:
+                    support((2 * b + ch + 5) // 2, (ch + 1) % 2)
+            if b + 4 < BLOCKS:
+                quantize_x(b + 4)
+            if b + 1 < BLOCKS:
+                full_max(b + 1)
+            if b >= 1 and b - 1 != batches[0][-1]:
+                add_up(b - 1, batch_of[b - 1])
+            if b == batches[0][-1]:
+                add_up(b, batches[0])
+                invert(batches[0], True)
+        order = [0, 1, 2, 7, 3, 4, 5, 6]
+        turn_back(0, 0)
+        turn_back(0, 1)
+        turn_back(1, 0)
+        turn_back(1, 1)
+        add_up(7, batches[2])
+        invert(batches[1], True)
+        for n, b in enumerate(order):
+            if b == 2:
+                invert(batches[2], False)
+            divide(b, 0)
+            divide(b, 1)
+            store(b)
+            if n + 2 < BLOCKS:
+                turn_back(order[n + 2], 0)
+                turn_back(order[n + 2], 1)

@@ -34,15 +34,17 @@ def tile_bcpnnhypercolumnrecall_kernel(tc, u, v, p, q, g, x_bytes, x_scale, out)
         psum = ctx.enter_context(tc.psum_pool(name="psum", bufs=1))
         ctx.enter_context(tc.manual_schedule())
 
-        banks_taken = []
+        banks_taken = {"cov": [], "x": [], "any": [], "z0": [], "z1": [], "turn": [], "late": []}
+        bank_order = {"any": (4, 5, 6, 7), "cov": (0, 1, 2, 3), "x": (5, 6, 7, 4, 1, 2), "z0": (0, 1, 2), "z1": (3, 4, 7, 3, 4, 5, 6, 7), "turn": (5, 6), "late": (3, 4, 2, 0, 1, 5, 6, 3, 4, 2, 0, 1, 5, 6, 3, 4)}
 
-        def next_bank(shape, dtype=F32):
-            tag = "bank_%d" % (len(banks_taken) % 7)
-            banks_taken.append(tag)
+        def next_bank(shape, dtype=F32, use="any"):
+            order = bank_order[use]
+            tag = "bank_%d" % order[len(banks_taken[use]) % len(order)]
+            banks_taken[use].append(tag)
             return psum.tile(list(shape), dtype, name=tag, tag=tag)
 
         def small_bank(shape):
-            return psum.tile(list(shape), F32, name="small", tag="small", bufs=1)
+            return psum.tile(list(shape), F32, name="small", tag="bank_7", bufs=1)
 
         def mx_tiles(name, width):
             codes = keep.tile([P, width], U32, name=name + "_codes", align_bytes=64)
@@ -89,23 +91,27 @@ def tile_bcpnnhypercolumnrecall_kernel(tc, u, v, p, q, g, x_bytes, x_scale, out)
         ident = keep.tile([P, P], F32, name="ident")
         ident_bf = keep.tile([P, P], BF16, name="ident_bf")
         make_identity(nc, ident[:])
-        nc.vector.tensor_copy(out=ident_bf[:], in_=ident[:])
+        make_identity(nc, ident_bf[:])
         log_q = keep.tile([P, C], F32, name="log_q")
         inv_q = keep.tile([P, C], F32, name="inv_q")
         nc.scalar.activation(out=log_q[:], in_=q_sb[:], func=ACT.Ln)
         nc.vector.reciprocal(out=inv_q[:], in_=q_sb[:])
         inv_q_rows = keep.tile([P, C, H], F32, name="inv_q_rows")
         inv_p = keep.tile([P, 2, PACK], F32, name="inv_p")
-        row_factor = keep.tile([P, 2, PACK], F32, name="row_factor")
         gain = keep.tile([P, 2, PACK], F32, name="gain")
 
-        def spread_inv_q():
+        spread = {}
+
+        def spread_inv_q_on_tensor():
             for ch in range(2):
-                bank = next_bank((P, 4, H))
+                spread[ch] = next_bank((P, 4, H))
                 for c in range(4):
                     column = inv_q[:, 4 * ch + c : 4 * ch + c + 1].to_broadcast([P, P])
-                    nc.tensor.transpose(bank[:, c, :], column, ident[:])
-                nc.scalar.copy(out=inv_q_rows[:, 4 * ch : 4 * ch + 4, :], in_=bank[:])
+                    nc.tensor.transpose(spread[ch][:, c, :], column, ident[:])
+
+        def collect_inv_q():
+            for ch in range(2):
+                nc.scalar.activation(out=inv_q_rows[:, 4 * ch : 4 * ch + 4, :], in_=spread[ch][:], func=ACT.Copy, scale=1.0 / T)
 
         def spread_x_scale():
             for ch in range(2):
@@ -120,8 +126,7 @@ def tile_bcpnnhypercolumnrecall_kernel(tc, u, v, p, q, g, x_bytes, x_scale, out)
 
         def row_constants():
             nc.vector.reciprocal(out=inv_p[:], in_=p_sb[:])
-            nc.vector.tensor_copy(out=gain[:], in_=g_sb[:])
-            nc.vector.tensor_scalar(out=row_factor[:], in0=inv_p[:], scalar1=1.0 / T, scalar2=None, op0=ALU.mult)
+            nc.scalar.copy(out=gain[:], in_=g_sb[:])
 
         u_mx = {}
         v_mx = {}
@@ -136,22 +141,24 @@ def tile_bcpnnhypercolumnrecall_kernel(tc, u, v, p, q, g, x_bytes, x_scale, out)
                     nc.tensor.matmul(out=bank[:, s, :], lhsT=ident_bf[:], rhs=moving, start=True, stop=True)
                 grouping[key, pair] = bank
 
+        def grouped_half(name, kh, half):
+            if (name, half) not in grouped:
+                grouped[name, half] = work.tile([P, 2 * HALF * PACK], BF16, name="grouped", tag="grouped", bufs=3, align_bytes=64)
+            return grouped[name, half][:, kh * HALF * PACK : (kh + 1) * HALF * PACK]
+
         def collect(*key):
-            tile = work.tile([P, HALF * PACK], BF16, name="grouped", tag="grouped", bufs=4, align_bytes=64)
+            tile = grouped_half(*key)
             for pair in range(2):
                 nc.scalar.copy(
                     out=tile[:, pair * 2 * BANK : (pair + 1) * 2 * BANK],
                     in_=grouping[key, pair][:].rearrange("p s n -> p (s n)"),
                 )
-            grouped[key] = tile
 
         def group_on_vector(key, raw):
-            tile = work.tile([P, HALF * PACK], BF16, name="grouped", tag="grouped", bufs=4, align_bytes=64)
             nc.vector.tensor_copy(
-                out=tile[:].rearrange("p (n i j) -> p n j i", i=4, j=PACK),
+                out=grouped_half(*key).rearrange("p (n i j) -> p n j i", i=4, j=PACK),
                 in_=raw[:].rearrange("p j (n i) -> p n j i", i=4),
             )
-            grouped[key] = tile
 
         def group_u(kh, ih):
             group_on_tensor(("u", kh, ih), u_raw[kh, ih], lambda t: slice(t, HALF, PACK))
@@ -159,13 +166,28 @@ def tile_bcpnnhypercolumnrecall_kernel(tc, u, v, p, q, g, x_bytes, x_scale, out)
         def group_v_on_tensor(kh, jh):
             group_on_tensor(("v", kh, jh), v_raw[kh, jh], lambda s: slice(s * P, (s + 1) * P))
 
-        def quantize_u(kh, ih):
-            u_mx[kh, ih] = mx_tiles("u_%d_%d" % (kh, ih), HALF)
-            quantize(u_mx[kh, ih], grouped["u", kh, ih][:])
+        def quantize_rows(name, store, half, first, count):
+            if half not in store:
+                store[half] = mx_tiles("%s_%d" % (name, half), 2 * HALF)
+            codes, scales = store[half]
+            cols = slice(first * HALF, (first + count) * HALF)
+            nc.vector.quantize_mx(
+                out=codes[:, cols].bitcast(FP8X4),
+                scales=scales[:, cols],
+                in_=grouped[name, half][:, first * HALF * PACK : (first + count) * HALF * PACK],
+            )
 
-        def quantize_v(kh, jh):
-            v_mx[kh, jh] = mx_tiles("v_%d_%d" % (kh, jh), HALF)
-            quantize(v_mx[kh, jh], grouped["v", kh, jh][:])
+        def quantize_u(ih, first=0, count=2):
+            quantize_rows("u", u_mx, ih, first, count)
+
+        def quantize_v(jh, first=0, count=2):
+            quantize_rows("v", v_mx, jh, first, count)
+
+        def group_u_on_scalar(kh, ih):
+            nc.scalar.copy(
+                out=grouped_half("u", kh, ih).rearrange("p (t m j) -> p t m j", t=PACK, j=PACK),
+                in_=u_raw[kh, ih][:].rearrange("p j (m t) -> p t m j", t=PACK),
+            )
 
         cov = {}
         ratio = {}
@@ -174,15 +196,16 @@ def tile_bcpnnhypercolumnrecall_kernel(tc, u, v, p, q, g, x_bytes, x_scale, out)
         w_mx = {}
 
         def covariance(ih, jh, t):
-            bank = next_bank((P, BANK))
-            cols = slice(t * P, (t + 1) * P)
+            bank = next_bank((P, BANK), use="cov")
             for kh in range(2):
+                u_cols = slice(kh * HALF + t * P, kh * HALF + (t + 1) * P)
+                v_cols = slice(kh * HALF, (kh + 1) * HALF)
                 nc.tensor.matmul_mx(
                     out=bank[:],
-                    lhsT=u_mx[kh, ih][0][:, cols].bitcast(FP8X4),
-                    lhsT_scale=u_mx[kh, ih][1][:, cols],
-                    rhs=v_mx[kh, jh][0][:].bitcast(FP8X4),
-                    rhs_scale=v_mx[kh, jh][1][:],
+                    lhsT=u_mx[ih][0][:, u_cols].bitcast(FP8X4),
+                    lhsT_scale=u_mx[ih][1][:, u_cols],
+                    rhs=v_mx[jh][0][:, v_cols].bitcast(FP8X4),
+                    rhs_scale=v_mx[jh][1][:, v_cols],
                     start=(kh == 0),
                     stop=(kh == 1),
                 )
@@ -194,7 +217,7 @@ def tile_bcpnnhypercolumnrecall_kernel(tc, u, v, p, q, g, x_bytes, x_scale, out)
             nc.vector.scalar_tensor_tensor(
                 out=ratio[ih, jh][:, t, :].rearrange("p (c h) -> p c h", c=C),
                 in0=cov[ih, jh, t][:].rearrange("p (h c) -> p c h", c=C),
-                scalar=row_factor[:, ih, t : t + 1],
+                scalar=inv_p[:, ih, t : t + 1],
                 in1=inv_q_rows[:, :, jh * (H // 2) : (jh + 1) * (H // 2)],
                 op0=ALU.mult,
                 op1=ALU.mult,
@@ -219,19 +242,37 @@ def tile_bcpnnhypercolumnrecall_kernel(tc, u, v, p, q, g, x_bytes, x_scale, out)
                     out=planes[ih, jh][:, t, :], in0=ratio[ih, jh][:, t, :], scalar1=factor, scalar2=None, op0=ALU.mult
                 )
 
-        def group_w(ih, jh, ch):
+        def group_w(ih, jh):
             if jh == 0:
-                w_grouped[ih, ch] = work.tile([P, 4, H, PACK], BF16, name="w_grouped", tag="w_grouped", bufs=4, align_bytes=64)
-            dst = w_grouped[ih, ch][:, :, jh * (H // 2) : (jh + 1) * (H // 2), :]
-            src = planes[ih, jh][:, :, ch * (HALF // 2) : (ch + 1) * (HALF // 2)]
+                w_grouped[ih] = work.tile([P, C, H, PACK], BF16, name="w_grouped", tag="w_grouped", bufs=2, align_bytes=64)
+            dst = w_grouped[ih][:, :, jh * (H // 2) : (jh + 1) * (H // 2), :]
             nc.vector.tensor_copy(
                 out=dst.rearrange("p c (n i) t -> p c n t i", i=4),
-                in_=src.rearrange("p t (c n i) -> p c n t i", c=4, i=4),
+                in_=planes[ih, jh][:].rearrange("p t (c n i) -> p c n t i", c=C, i=4),
             )
 
-        def quantize_w(ih, ch):
-            w_mx[ih, ch] = mx_tiles("w_%d_%d" % (ih, ch), 4 * H)
-            quantize(w_mx[ih, ch], w_grouped[ih, ch][:].rearrange("p c h t -> p (c h t)"))
+        def group_w_on_tensor(ih, jh):
+            for pair in range(2):
+                bank = next_bank((P, 2, BANK), BF16, use="cov")
+                for s in range(2):
+                    cols = slice((2 * pair + s) * P, (2 * pair + s + 1) * P)
+                    moving = planes[ih, jh][:, :, cols].rearrange("p t n -> p n t")
+                    nc.tensor.matmul(out=bank[:, s, :], lhsT=ident_bf[:], rhs=moving, start=True, stop=True)
+                grouping[("w", ih, jh), pair] = bank
+
+        def collect_w(ih, jh):
+            if jh == 0:
+                w_grouped[ih] = work.tile([P, C, H, PACK], BF16, name="w_grouped", tag="w_grouped", bufs=2, align_bytes=64)
+            for pair in range(2):
+                dst = w_grouped[ih][:, 4 * pair : 4 * pair + 4, jh * (H // 2) : (jh + 1) * (H // 2), :]
+                nc.scalar.copy(
+                    out=dst.rearrange("p c h t -> p c (h t)"),
+                    in_=grouping[("w", ih, jh), pair][:].rearrange("p s (c n) -> p (s c) n", c=2),
+                )
+
+        def quantize_w(ih):
+            w_mx[ih] = mx_tiles("w_%d" % ih, C * H)
+            quantize(w_mx[ih], w_grouped[ih][:].rearrange("p c h t -> p (c h t)"))
 
         x_value = {}
         x_turned = {}
@@ -244,7 +285,7 @@ def tile_bcpnnhypercolumnrecall_kernel(tc, u, v, p, q, g, x_bytes, x_scale, out)
 
         def turn_x(b):
             words = x_value[b][:].bitcast(F32)
-            bank = next_bank((P, 2, 2, P))
+            bank = next_bank((P, 2, 2, P), use="x")
             for ih in range(2):
                 for w in range(2):
                     nc.tensor.transpose(bank[:, ih, w, :], words[:, 256 * ih + w : 256 * (ih + 1) : 2], ident[:])
@@ -252,18 +293,21 @@ def tile_bcpnnhypercolumnrecall_kernel(tc, u, v, p, q, g, x_bytes, x_scale, out)
 
         def collect_x(b):
             bank = x_turned[b]
-            x_grouped[b] = work.tile([P, N], BF16, name="x_grouped", tag="x_grouped", bufs=6, align_bytes=64)
+            if b % 2 == 0:
+                x_grouped[b // 2] = work.tile([P, 2 * N], BF16, name="x_grouped", tag="x_grouped", bufs=3, align_bytes=64)
+            dst = x_grouped[b // 2][:, (b % 2) * N : (b % 2 + 1) * N]
             nc.scalar.copy(
-                out=x_grouped[b][:].bitcast(F32).rearrange("p (a r w) -> p a r w", a=2, w=2),
+                out=dst.bitcast(F32).rearrange("p (a r w) -> p a r w", a=2, w=2),
                 in_=bank[:].rearrange("p a w r -> p a r w"),
             )
 
-        def quantize_x(b):
-            x_mx[b] = mx_tiles("x_%d" % b, 2 * P)
-            quantize(x_mx[b], x_grouped[b][:])
+        def quantize_x(pair):
+            x_mx[pair] = mx_tiles("x_%d" % pair, 4 * P)
+            quantize(x_mx[pair], x_grouped[pair][:])
 
         z = {}
         top = {}
+        parked = {}
         shifted = {}
         expd = {}
         turned = {}
@@ -273,63 +317,73 @@ def tile_bcpnnhypercolumnrecall_kernel(tc, u, v, p, q, g, x_bytes, x_scale, out)
 
         def support(b, ch):
             if True:
-                bank = next_bank((P, 4, P))
+                bank = next_bank((P, 4, P), use="z%d" % ch)
                 for c in range(4):
-                    cols = slice(c * H, (c + 1) * H)
+                    cols = slice((4 * ch + c) * H, (4 * ch + c + 1) * H)
                     for ih in range(2):
-                        rows = slice(ih * P, (ih + 1) * P)
+                        rows = slice((2 * (b % 2) + ih) * P, (2 * (b % 2) + ih + 1) * P)
                         nc.tensor.matmul_mx(
                             out=bank[:, c, :],
-                            lhsT=w_mx[ih, ch][0][:, cols].bitcast(FP8X4),
-                            lhsT_scale=w_mx[ih, ch][1][:, cols],
-                            rhs=x_mx[b][0][:, rows].bitcast(FP8X4),
-                            rhs_scale=x_mx[b][1][:, rows],
+                            lhsT=w_mx[ih][0][:, cols].bitcast(FP8X4),
+                            lhsT_scale=w_mx[ih][1][:, cols],
+                            rhs=x_mx[b // 2][0][:, rows].bitcast(FP8X4),
+                            rhs_scale=x_mx[b // 2][1][:, rows],
                             start=(ih == 0),
                             stop=(ih == 1),
                         )
                 z[b, ch] = bank
 
-        def half_max(b, ch):
-            if ch == 0:
-                top[b] = work.tile([P, 3, P], F32, name="top", tag="top", bufs=3)
-            nc.vector.tensor_reduce(out=top[b][:, ch, :], in_=z[b, ch][:].rearrange("p c r -> p r c"), axis=AXIS.X, op=ALU.max)
+        def park(b):
+            parked[b] = work.tile([P, 4, P], F32, name="parked", tag="x_value", bufs=8)
+            nc.scalar.copy(out=parked[b][:], in_=z[b, 1][:])
 
-        def full_max(b):
-            nc.vector.tensor_tensor(out=top[b][:, 2, :], in0=top[b][:, 0, :], in1=top[b][:, 1, :], op=ALU.max)
+        def max_of_pairs(b):
+            top[b] = work.tile([P, 5, P], F32, name="top", tag="top", bufs=3)
+            nc.vector.tensor_tensor(out=top[b][:, 0:4, :], in0=z[b, 0][:], in1=parked[b][:], op=ALU.max)
 
-        def shift(b, ch):
-            if ch == 0:
-                shifted[b] = work.tile([P, C, P], F32, name="shifted", tag="shifted", bufs=3)
-            nc.vector.tensor_tensor(
-                out=shifted[b][:, 4 * ch : 4 * ch + 4, :],
-                in0=z[b, ch][:],
-                in1=top[b][:, 2:3, :].broadcast_to([P, 4, P]),
+        def max_of_units(b):
+            nc.vector.tensor_reduce(
+                out=top[b][:, 4, :], in_=top[b][:, 0:4, :].rearrange("p c r -> p r c"), axis=AXIS.X, op=ALU.max
+            )
+
+        def shift(b, ch, engine):
+            if b // 2 not in shifted:
+                shifted[b // 2] = work.tile([P, C, 2, P], F32, name="shifted", tag="ratio", bufs=3)
+            engine.tensor_tensor(
+                out=shifted[b // 2][:, 4 * ch : 4 * ch + 4, b % 2, :],
+                in0=parked[b][:] if ch == 1 else z[b, ch][:],
+                in1=top[b][:, 4:5, :].broadcast_to([P, 4, P]),
                 op=ALU.subtract,
             )
 
-        def exponentiate(b, ch):
-            if ch == 0:
-                expd[b] = work.tile([P, C, P], F32, name="expd", tag="wide", bufs=8)
-            for c in range(4 * ch, 4 * ch + 4):
-                nc.scalar.activation(out=expd[b][:, c, :], in_=shifted[b][:, c, :], func=ACT.Exp, bias=log_q[:, c : c + 1])
+        def exponentiate(pair):
+            for c in range(C):
+                if c % 4 == 0:
+                    expd[pair, c // 4] = work.tile([P, 4, 2, P], F32, name="expd", tag="wide", bufs=8)
+                nc.scalar.activation(
+                    out=expd[pair, c // 4][:, c % 4, :, :],
+                    in_=shifted[pair][:, c, :, :],
+                    func=ACT.Exp,
+                    bias=log_q[:, c : c + 1],
+                )
 
         def add_up(b, batch):
             if b == batch[0]:
-                sums[batch] = small_bank((P, len(batch), H)) if len(batch) > 1 else next_bank((P, 1, H))
+                sums[batch] = small_bank((P, len(batch), H)) if len(batch) > 1 else next_bank((P, 1, H), use="late")
             for c in range(C):
                 nc.tensor.matmul(
                     out=sums[batch][:, b - batch[0], :],
-                    lhsT=expd[b][:, c, :],
+                    lhsT=expd[b // 2, c // 4][:, c % 4, b % 2, :],
                     rhs=ident[:],
                     start=(c == 0),
                     stop=(c == C - 1),
                     is_transpose=True,
                 )
 
-        def turn_back(b, ch):
-            bank = next_bank((P, 4, H))
+        def turn_back(b, ch, use="turn"):
+            bank = next_bank((P, 4, H), use=use)
             for c in range(4):
-                nc.tensor.transpose(bank[:, c, :], expd[b][:, 4 * ch + c, :], ident[:])
+                nc.tensor.transpose(bank[:, c, :], expd[b // 2, ch][:, c, b % 2, :], ident[:])
             turned[b, ch] = bank
 
         def invert(batch, on_scalar):
@@ -344,7 +398,7 @@ def tile_bcpnnhypercolumnrecall_kernel(tc, u, v, p, q, g, x_bytes, x_scale, out)
 
         def divide(b, ch):
             if ch == 0:
-                result[b] = work.tile([P, H, C], F32, name="result", tag="result", bufs=4)
+                result[b] = work.tile([P, H, C], F32, name="result", tag="result", bufs=5)
             nc.vector.tensor_tensor(
                 out=result[b][:, :, 4 * ch : 4 * ch + 4],
                 in0=turned[b, ch][:].rearrange("p c h -> p h c"),
@@ -368,56 +422,52 @@ def tile_bcpnnhypercolumnrecall_kernel(tc, u, v, p, q, g, x_bytes, x_scale, out)
                 apply_gain(*units[k], t, on_scalar)
 
         spread_x_scale()
-        group_u(0, 0)
-        collect("u", 0, 0)
+        group_u_on_scalar(0, 0)
         scale_x(0)
-        scale_x(1)
-        group_u(1, 0)
-        collect("u", 1, 0)
-        spread_inv_q()
+        spread_inv_q_on_tensor()
+        group_u_on_scalar(1, 0)
         group_on_vector(("v", 0, 0), v_raw[0, 0])
-        quantize_u(0, 0)
-        quantize_v(0, 0)
         group_on_vector(("v", 1, 0), v_raw[1, 0])
-        quantize_u(1, 0)
-        row_constants()
-        quantize_v(1, 0)
+        collect_inv_q()
+        quantize_v(0)
+        quantize_u(0)
         group_v_on_tensor(0, 1)
+        row_constants()
         collect("v", 0, 1)
         covariances(0)
-        quantize_v(0, 1)
+        group_v_on_tensor(1, 1)
         normalise(0, 0, 0)
         normalise(0, 0, 1)
         clamp(0, 0, 0, 2)
-        group_v_on_tensor(1, 1)
         normalise(0, 0, 2)
         normalise(0, 0, 3)
         group_u(0, 1)
+        quantize_v(1, 0, 1)
+        scale_x(1)
         clamp(0, 0, 2, 2)
         collect("v", 1, 1)
-        logarithm(0, 0, 0, 2)
-        scale_x(2)
-        quantize_v(1, 1)
+        quantize_v(1, 1, 1)
         covariances(1)
-        scale_x(3)
+        logarithm(0, 0, 0, 2)
         logarithm(0, 0, 2, 2)
         collect("u", 0, 1)
         group_u(1, 1)
+        scale_x(2)
         normalise(0, 1, 0)
         normalise(0, 1, 1)
         clamp(0, 1, 0, 2)
         normalise(0, 1, 2)
         normalise(0, 1, 3)
-        collect("u", 1, 1)
         clamp(0, 1, 2, 2)
+        collect("u", 1, 1)
+        quantize_u(1, 0, 1)
         gains(0, (0, 1, 2, 3), False)
-        quantize_u(0, 1)
+        quantize_u(1, 1, 1)
+        covariances(2)
         logarithm(0, 1, 0, 2)
         logarithm(0, 1, 2, 2)
-        group_w(0, 0, 0)
-        quantize_u(1, 1)
-        covariances(2)
-        group_w(0, 0, 1)
+        group_w(0, 0)
+        gains(1, (0, 1), True)
         normalise(1, 0, 0)
         normalise(1, 0, 1)
         clamp(1, 0, 0, 2)
@@ -425,94 +475,128 @@ def tile_bcpnnhypercolumnrecall_kernel(tc, u, v, p, q, g, x_bytes, x_scale, out)
         normalise(1, 0, 3)
         clamp(1, 0, 2, 2)
         covariances(3)
-        gains(1, (0, 1, 2, 3), False)
-        logarithm(1, 0, 0, 2)
-        logarithm(1, 0, 2, 2)
-        normalise(1, 1, 0)
-        normalise(1, 1, 1)
-        clamp(1, 1, 0, 2)
-        normalise(1, 1, 2)
-        normalise(1, 1, 3)
         turn_x(0)
         turn_x(1)
+        turn_x(2)
+        scale_x(3)
+        logarithm(1, 0, 0, 2)
+        logarithm(1, 0, 2, 2)
+        for t in range(PACK):
+            normalise(1, 1, t)
+        turn_x(3)
+        gains(1, (2, 3), True)
+        clamp(1, 1, 0, 2)
         clamp(1, 1, 2, 2)
-        group_w(0, 1, 0)
-        group_w(0, 1, 1)
+        scale_x(4)
+        turn_x(4)
+        group_w(0, 1)
+        gains(2, (0, 1), True)
         logarithm(1, 1, 0, 2)
         logarithm(1, 1, 2, 2)
-        gains(2, (0, 1), False)
-        gains(2, (2, 3), True)
-        gains(3, (0, 1, 2, 3), True)
-        quantize_w(0, 0)
-        quantize_w(0, 1)
-        scale_x(4)
+        gains(2, (2, 3), False)
+        quantize_w(0)
         scale_x(5)
-        group_w(1, 0, 0)
-        group_w(1, 0, 1)
+        turn_x(5)
+        group_w(1, 0)
+        gains(3, (2, 3), True)
+        gains(3, (0, 1), False)
         collect_x(0)
         collect_x(1)
-        turn_x(2)
-        turn_x(3)
-        turn_x(4)
-        turn_x(5)
         scale_x(6)
-        group_w(1, 1, 0)
-        group_w(1, 1, 1)
-        quantize_x(0)
-        quantize_w(1, 0)
-        quantize_w(1, 1)
-        support(0, 0)
-        support(0, 1)
+        turn_x(6)
+        group_w(1, 1)
         for b in range(2, 6):
             collect_x(b)
-        turn_x(6)
-        quantize_x(1)
+        quantize_x(0)
+        quantize_w(1)
+        support(0, 1)
+        support(0, 0)
         scale_x(7)
-        support(1, 0)
-        support(1, 1)
         collect_x(6)
+        park(0)
         turn_x(7)
+        support(1, 1)
+        support(1, 0)
+        quantize_x(1)
         collect_x(7)
-        quantize_x(2)
+        park(1)
 
-        batches = [(0, 1, 2), (3, 4, 5, 6), (7,)]
-        batch_of = {b: batch for batch in batches for b in batch}
+        early, late = (0, 1, 2, 3), (4, 5)
 
-        half_max(0, 0)
-        half_max(0, 1)
-        support(2, 0)
-        quantize_x(3)
-        full_max(0)
-        for b in range(BLOCKS):
-            for ch in range(2):
-                if b + 1 < BLOCKS:
-                    half_max(b + 1, ch)
-                shift(b, ch)
-                exponentiate(b, ch)
-                if 2 * b + ch + 5 < 2 * BLOCKS:
-                    support((2 * b + ch + 5) // 2, (ch + 1) % 2)
-            if b + 4 < BLOCKS:
-                quantize_x(b + 4)
-            if b + 1 < BLOCKS:
-                full_max(b + 1)
-            if b >= 1 and b - 1 != batches[0][-1]:
-                add_up(b - 1, batch_of[b - 1])
-            if b == batches[0][-1]:
-                add_up(b, batches[0])
-                invert(batches[0], True)
-        order = [0, 1, 2, 7, 3, 4, 5, 6]
-        turn_back(0, 0)
-        turn_back(0, 1)
-        turn_back(1, 0)
-        turn_back(1, 1)
-        add_up(7, batches[2])
-        invert(batches[1], True)
-        for n, b in enumerate(order):
-            if b == 2:
-                invert(batches[2], False)
+        def ahead(b):
+            support(b, 1)
+            park(b)
+
+        def turn_both(b, use="late"):
+            turn_back(b, 0, use)
+            turn_back(b, 1, use)
+
+        def finish(b):
             divide(b, 0)
             divide(b, 1)
             store(b)
-            if n + 2 < BLOCKS:
-                turn_back(order[n + 2], 0)
-                turn_back(order[n + 2], 1)
+
+        max_of_pairs(0)
+        ahead(2)
+        ahead(3)
+        quantize_x(2)
+        max_of_units(0)
+        ahead(4)
+        support(2, 0)
+        quantize_x(3)
+        for d in (5, 6, 7):
+            support(d, 1)
+        for b in range(BLOCKS):
+            last = b + 1 == BLOCKS
+            on_gpsimd = True and not last
+            if on_gpsimd:
+                shift(b, 1, nc.gpsimd)
+            if not last:
+                max_of_pairs(b + 1)
+            shift(b, 0, nc.vector)
+            if b + 3 < BLOCKS:
+                support(b + 3, 0)
+            if not last:
+                max_of_units(b + 1)
+            if not on_gpsimd:
+                shift(b, 1, nc.vector)
+            if b in (1, 3):
+                exponentiate(b // 2)
+            if b == 1:
+                for d in (5, 6, 7):
+                    park(d)
+            if b == 3:
+                add_up(0, early)
+                add_up(1, early)
+            if b == 4:
+                add_up(2, early)
+                add_up(3, early)
+                invert(early, True)
+                turn_both(0, "turn")
+                turn_both(1)
+        exponentiate(3)
+        exponentiate(2)
+        turn_both(2)
+        turn_back(3, 0, "late")
+        divide(0, 0)
+        turn_back(3, 1, "late")
+        divide(0, 1)
+        store(0)
+        add_up(6, (6,))
+        finish(1)
+        add_up(7, (7,))
+        finish(2)
+        turn_both(6)
+        finish(3)
+        turn_both(7)
+        add_up(4, late)
+        add_up(5, late)
+        invert(late, True)
+        invert((6,), False)
+        invert((7,), False)
+        finish(6)
+        turn_both(4)
+        turn_both(5)
+        finish(7)
+        finish(4)
+        finish(5)

from contextlib import ExitStack

import concourse.mybir as mybir
from concourse.masks import make_identity

T, N, M, R, C = 1024, 1024, 1024, 1024, 8
H = M // C
FLOOR = 0.1
FLOPS = 2 * T * N * M + 2 * R * N * M

F32 = mybir.dt.float32
BF16 = mybir.dt.bfloat16
U32 = mybir.dt.uint32
U8 = mybir.dt.uint8
FP8 = mybir.dt.float8_e4m3fn
FP8X4 = mybir.dt.float8_e4m3fn_x4
ALU = mybir.AluOpType
ACT = mybir.ActivationFunctionType
AXIS = mybir.AxisListType

P = 128
PACK = 4
KP = P * PACK
BANK = 512
HALF = 512
BLOCKS = R // P


def tile_bcpnnhypercolumnrecall_kernel(tc, u, v, p, q, g, x_bytes, x_scale, out):
    nc = tc.nc
    with ExitStack() as ctx:
        keep = ctx.enter_context(tc.tile_pool(name="keep", bufs=1))
        work = ctx.enter_context(tc.tile_pool(name="work", bufs=2))
        psum = ctx.enter_context(tc.psum_pool(name="psum", bufs=1))
        ctx.enter_context(tc.manual_schedule())

        banks_taken = {"cov": [], "x": [], "any": [], "z0": [], "z1": [], "turn": [], "late": []}
        bank_order = {"any": (4, 5, 6, 7), "cov": (0, 1, 2, 3), "x": (5, 6, 7, 4, 1, 2), "z0": (0, 1, 2), "z1": (3, 4, 7, 3, 4, 5, 6, 7), "turn": (5, 6), "late": (3, 4, 2, 0, 1, 5, 6, 3, 4, 2, 0, 1, 5, 6, 3, 4)}

        def next_bank(shape, dtype=F32, use="any"):
            order = bank_order[use]
            tag = "bank_%d" % order[len(banks_taken[use]) % len(order)]
            banks_taken[use].append(tag)
            return psum.tile(list(shape), dtype, name=tag, tag=tag)

        def small_bank(shape):
            return psum.tile(list(shape), F32, name="small", tag="bank_7", bufs=1)

        def mx_tiles(name, width):
            codes = keep.tile([P, width], U32, name=name + "_codes", align_bytes=64)
            scales = keep.tile([P, width], U8, name=name + "_scales", align_bytes=64)
            return codes, scales

        def quantize(dst, src):
            nc.vector.quantize_mx(out=dst[0][:].bitcast(FP8X4), scales=dst[1][:], in_=src)

        def load_rows(name, src, kh, half):
            raw = work.tile([P, PACK, HALF], BF16, name="raw", tag="wide", bufs=8)
            rows = src[kh * KP : (kh + 1) * KP, half * HALF : (half + 1) * HALF]
            nc.sync.dma_start(out=raw[:], in_=rows.rearrange("(p j) n -> p j n", j=PACK))
            return raw

        def load_x(first, count):
            xb = keep.tile([P, count, N], U8, name="x_bytes_%d" % first)
            rows = x_bytes[first * P : (first + count) * P, :]
            nc.sync.dma_start(out=xb[:], in_=rows.rearrange("(b p) k -> p b k", p=P))
            return [xb[:, b, :] for b in range(count)]

        q_sb = keep.tile([P, C], BF16, name="q_sb")
        p_sb = keep.tile([P, 2, PACK], BF16, name="p_sb")
        g_sb = keep.tile([P, 2, PACK], BF16, name="g_sb")
        x_scales = keep.tile([P, N], F32, name="x_scales")
        u_raw = {}
        v_raw = {}
        s_sb = keep.tile([P, C], F32, name="s_sb")
        nc.sync.dma_start(out=s_sb[:], in_=x_scale.rearrange("o (a b) -> (o a) b", b=C))
        nc.sync.dma_start(out=q_sb[:], in_=q.rearrange("(h c) -> h c", c=C))
        x_rows = load_x(0, 2)
        u_raw[0, 0] = load_rows("u", u, 0, 0)
        u_raw[1, 0] = load_rows("u", u, 1, 0)
        v_raw[0, 0] = load_rows("v", v, 0, 0)
        v_raw[1, 0] = load_rows("v", v, 1, 0)
        nc.sync.dma_start(out=p_sb[:], in_=p.rearrange("(a p t) -> p a t", p=P, t=PACK))
        nc.sync.dma_start(out=g_sb[:], in_=g.rearrange("(a p t) -> p a t", p=P, t=PACK))
        v_raw[0, 1] = load_rows("v", v, 0, 1)
        v_raw[1, 1] = load_rows("v", v, 1, 1)
        u_raw[0, 1] = load_rows("u", u, 0, 1)
        u_raw[1, 1] = load_rows("u", u, 1, 1)
        x_rows = x_rows + load_x(2, BLOCKS - 2)

        ident = keep.tile([P, P], F32, name="ident")
        ident_bf = keep.tile([P, P], BF16, name="ident_bf")
        make_identity(nc, ident[:])
        make_identity(nc, ident_bf[:])
        log_q = keep.tile([P, C], F32, name="log_q")
        inv_q = keep.tile([P, C], F32, name="inv_q")
        nc.scalar.activation(out=log_q[:], in_=q_sb[:], func=ACT.Ln)
        nc.vector.reciprocal(out=inv_q[:], in_=q_sb[:])
        inv_q_rows = keep.tile([P, C, H], F32, name="inv_q_rows")
        inv_p = keep.tile([P, 2, PACK], F32, name="inv_p")
        gain = keep.tile([P, 2, PACK], F32, name="gain")

        spread = {}

        def spread_inv_q_on_tensor():
            for ch in range(2):
                spread[ch] = next_bank((P, 4, H))
                for c in range(4):
                    column = inv_q[:, 4 * ch + c : 4 * ch + c + 1].to_broadcast([P, P])
                    nc.tensor.transpose(spread[ch][:, c, :], column, ident[:])

        def collect_inv_q():
            for ch in range(2):
                nc.scalar.activation(out=inv_q_rows[:, 4 * ch : 4 * ch + 4, :], in_=spread[ch][:], func=ACT.Copy, scale=1.0 / T)

        def spread_x_scale():
            for ch in range(2):
                bank = next_bank((P, 4, P))
                for b in range(4):
                    column = s_sb[:, 4 * ch + b : 4 * ch + b + 1].to_broadcast([P, P])
                    nc.tensor.transpose(bank[:, b, :], column, ident[:])
                nc.scalar.copy(
                    out=x_scales[:].rearrange("p (a b) -> p a b", b=C)[:, :, 4 * ch : 4 * ch + 4],
                    in_=bank[:].rearrange("p b a -> p a b"),
                )

        def row_constants():
            nc.vector.reciprocal(out=inv_p[:], in_=p_sb[:])
            nc.scalar.copy(out=gain[:], in_=g_sb[:])

        u_mx = {}
        v_mx = {}
        grouped = {}
        grouping = {}

        def group_on_tensor(key, raw, columns):
            for pair in range(2):
                bank = next_bank((P, 2, BANK), BF16)
                for s in range(2):
                    moving = raw[:, :, columns(2 * pair + s)].rearrange("p j n -> p n j")
                    nc.tensor.matmul(out=bank[:, s, :], lhsT=ident_bf[:], rhs=moving, start=True, stop=True)
                grouping[key, pair] = bank

        def grouped_half(name, kh, half):
            if (name, half) not in grouped:
                grouped[name, half] = work.tile([P, 2 * HALF * PACK], BF16, name="grouped", tag="grouped", bufs=3, align_bytes=64)
            return grouped[name, half][:, kh * HALF * PACK : (kh + 1) * HALF * PACK]

        def collect(*key):
            tile = grouped_half(*key)
            for pair in range(2):
                nc.scalar.copy(
                    out=tile[:, pair * 2 * BANK : (pair + 1) * 2 * BANK],
                    in_=grouping[key, pair][:].rearrange("p s n -> p (s n)"),
                )

        def group_on_vector(key, raw):
            nc.vector.tensor_copy(
                out=grouped_half(*key).rearrange("p (n i j) -> p n j i", i=4, j=PACK),
                in_=raw[:].rearrange("p j (n i) -> p n j i", i=4),
            )

        def group_u(kh, ih):
            group_on_tensor(("u", kh, ih), u_raw[kh, ih], lambda t: slice(t, HALF, PACK))

        def group_v_on_tensor(kh, jh):
            group_on_tensor(("v", kh, jh), v_raw[kh, jh], lambda s: slice(s * P, (s + 1) * P))

        def quantize_rows(name, store, half, first, count):
            if half not in store:
                store[half] = mx_tiles("%s_%d" % (name, half), 2 * HALF)
            codes, scales = store[half]
            cols = slice(first * HALF, (first + count) * HALF)
            nc.vector.quantize_mx(
                out=codes[:, cols].bitcast(FP8X4),
                scales=scales[:, cols],
                in_=grouped[name, half][:, first * HALF * PACK : (first + count) * HALF * PACK],
            )

        def quantize_u(ih, first=0, count=2):
            quantize_rows("u", u_mx, ih, first, count)

        def quantize_v(jh, first=0, count=2):
            quantize_rows("v", v_mx, jh, first, count)

        def group_u_on_scalar(kh, ih):
            nc.scalar.copy(
                out=grouped_half("u", kh, ih).rearrange("p (t m j) -> p t m j", t=PACK, j=PACK),
                in_=u_raw[kh, ih][:].rearrange("p j (m t) -> p t m j", t=PACK),
            )

        cov = {}
        ratio = {}
        planes = {}
        w_grouped = {}
        w_mx = {}

        def covariance(ih, jh, t):
            bank = next_bank((P, BANK), use="cov")
            for kh in range(2):
                u_cols = slice(kh * HALF + t * P, kh * HALF + (t + 1) * P)
                v_cols = slice(kh * HALF, (kh + 1) * HALF)
                nc.tensor.matmul_mx(
                    out=bank[:],
                    lhsT=u_mx[ih][0][:, u_cols].bitcast(FP8X4),
                    lhsT_scale=u_mx[ih][1][:, u_cols],
                    rhs=v_mx[jh][0][:, v_cols].bitcast(FP8X4),
                    rhs_scale=v_mx[jh][1][:, v_cols],
                    start=(kh == 0),
                    stop=(kh == 1),
                )
            cov[ih, jh, t] = bank

        def normalise(ih, jh, t):
            if t == 0:
                ratio[ih, jh] = work.tile([P, PACK, HALF], F32, name="ratio", tag="ratio", bufs=3)
            nc.vector.scalar_tensor_tensor(
                out=ratio[ih, jh][:, t, :].rearrange("p (c h) -> p c h", c=C),
                in0=cov[ih, jh, t][:].rearrange("p (h c) -> p c h", c=C),
                scalar=inv_p[:, ih, t : t + 1],
                in1=inv_q_rows[:, :, jh * (H // 2) : (jh + 1) * (H // 2)],
                op0=ALU.mult,
                op1=ALU.mult,
            )

        def clamp(ih, jh, first, count):
            part = ratio[ih, jh][:, first : first + count, :]
            nc.scalar.activation(out=part, in_=part, func=ACT.Relu, bias=1.0 - FLOOR)

        def logarithm(ih, jh, first, count):
            part = ratio[ih, jh][:, first : first + count, :]
            nc.scalar.activation(out=part, in_=part, func=ACT.Ln, bias=FLOOR)

        def apply_gain(ih, jh, t, on_scalar):
            if (ih, jh) not in planes:
                planes[ih, jh] = work.tile([P, PACK, HALF], BF16, name="planes", tag="planes", bufs=2)
            factor = gain[:, ih, t : t + 1]
            if on_scalar:
                nc.scalar.activation(out=planes[ih, jh][:, t, :], in_=ratio[ih, jh][:, t, :], func=ACT.Copy, scale=factor)
            else:
                nc.vector.tensor_scalar(
                    out=planes[ih, jh][:, t, :], in0=ratio[ih, jh][:, t, :], scalar1=factor, scalar2=None, op0=ALU.mult
                )

        def group_w(ih, jh):
            if jh == 0:
                w_grouped[ih] = work.tile([P, C, H, PACK], BF16, name="w_grouped", tag="w_grouped", bufs=2, align_bytes=64)
            dst = w_grouped[ih][:, :, jh * (H // 2) : (jh + 1) * (H // 2), :]
            nc.vector.tensor_copy(
                out=dst.rearrange("p c (n i) t -> p c n t i", i=4),
                in_=planes[ih, jh][:].rearrange("p t (c n i) -> p c n t i", c=C, i=4),
            )

        def group_w_on_tensor(ih, jh):
            for pair in range(2):
                bank = next_bank((P, 2, BANK), BF16, use="cov")
                for s in range(2):
                    cols = slice((2 * pair + s) * P, (2 * pair + s + 1) * P)
                    moving = planes[ih, jh][:, :, cols].rearrange("p t n -> p n t")
                    nc.tensor.matmul(out=bank[:, s, :], lhsT=ident_bf[:], rhs=moving, start=True, stop=True)
                grouping[("w", ih, jh), pair] = bank

        def collect_w(ih, jh):
            if jh == 0:
                w_grouped[ih] = work.tile([P, C, H, PACK], BF16, name="w_grouped", tag="w_grouped", bufs=2, align_bytes=64)
            for pair in range(2):
                dst = w_grouped[ih][:, 4 * pair : 4 * pair + 4, jh * (H // 2) : (jh + 1) * (H // 2), :]
                nc.scalar.copy(
                    out=dst.rearrange("p c h t -> p c (h t)"),
                    in_=grouping[("w", ih, jh), pair][:].rearrange("p s (c n) -> p (s c) n", c=2),
                )

        def quantize_w(ih):
            w_mx[ih] = mx_tiles("w_%d" % ih, C * H)
            quantize(w_mx[ih], w_grouped[ih][:].rearrange("p c h t -> p (c h t)"))

        x_value = {}
        x_turned = {}
        x_grouped = {}
        x_mx = {}

        def scale_x(b):
            x_value[b] = work.tile([P, N], BF16, name="x_value", tag="x_value", bufs=8)
            nc.vector.tensor_tensor(out=x_value[b][:], in0=x_rows[b].bitcast(FP8), in1=x_scales[:], op=ALU.mult)

        def turn_x(b):
            words = x_value[b][:].bitcast(F32)
            bank = next_bank((P, 2, 2, P), use="x")
            for ih in range(2):
                for w in range(2):
                    nc.tensor.transpose(bank[:, ih, w, :], words[:, 256 * ih + w : 256 * (ih + 1) : 2], ident[:])
            x_turned[b] = bank

        def collect_x(b):
            bank = x_turned[b]
            if b % 2 == 0:
                x_grouped[b // 2] = work.tile([P, 2 * N], BF16, name="x_grouped", tag="x_grouped", bufs=3, align_bytes=64)
            dst = x_grouped[b // 2][:, (b % 2) * N : (b % 2 + 1) * N]
            nc.scalar.copy(
                out=dst.bitcast(F32).rearrange("p (a r w) -> p a r w", a=2, w=2),
                in_=bank[:].rearrange("p a w r -> p a r w"),
            )

        def quantize_x(pair):
            x_mx[pair] = mx_tiles("x_%d" % pair, 4 * P)
            quantize(x_mx[pair], x_grouped[pair][:])

        z = {}
        top = {}
        parked = {}
        shifted = {}
        expd = {}
        turned = {}
        sums = {}
        inv_sum = {}
        result = {}

        def support(b, ch):
            if True:
                bank = next_bank((P, 4, P), use="z%d" % ch)
                for c in range(4):
                    cols = slice((4 * ch + c) * H, (4 * ch + c + 1) * H)
                    for ih in range(2):
                        rows = slice((2 * (b % 2) + ih) * P, (2 * (b % 2) + ih + 1) * P)
                        nc.tensor.matmul_mx(
                            out=bank[:, c, :],
                            lhsT=w_mx[ih][0][:, cols].bitcast(FP8X4),
                            lhsT_scale=w_mx[ih][1][:, cols],
                            rhs=x_mx[b // 2][0][:, rows].bitcast(FP8X4),
                            rhs_scale=x_mx[b // 2][1][:, rows],
                            start=(ih == 0),
                            stop=(ih == 1),
                        )
                z[b, ch] = bank

        def park(b):
            parked[b] = work.tile([P, 4, P], F32, name="parked", tag="x_value", bufs=8)
            nc.scalar.copy(out=parked[b][:], in_=z[b, 1][:])

        def max_of_pairs(b):
            top[b] = work.tile([P, 5, P], F32, name="top", tag="top", bufs=3)
            nc.vector.tensor_tensor(out=top[b][:, 0:4, :], in0=z[b, 0][:], in1=parked[b][:], op=ALU.max)

        def max_of_units(b):
            nc.vector.tensor_reduce(
                out=top[b][:, 4, :], in_=top[b][:, 0:4, :].rearrange("p c r -> p r c"), axis=AXIS.X, op=ALU.max
            )

        def shift(b, ch, engine):
            if b // 2 not in shifted:
                shifted[b // 2] = work.tile([P, C, 2, P], F32, name="shifted", tag="ratio", bufs=3)
            engine.tensor_tensor(
                out=shifted[b // 2][:, 4 * ch : 4 * ch + 4, b % 2, :],
                in0=parked[b][:] if ch == 1 else z[b, ch][:],
                in1=top[b][:, 4:5, :].broadcast_to([P, 4, P]),
                op=ALU.subtract,
            )

        def exponentiate(pair):
            for c in range(C):
                if c % 4 == 0:
                    expd[pair, c // 4] = work.tile([P, 4, 2, P], F32, name="expd", tag="wide", bufs=8)
                nc.scalar.activation(
                    out=expd[pair, c // 4][:, c % 4, :, :],
                    in_=shifted[pair][:, c, :, :],
                    func=ACT.Exp,
                    bias=log_q[:, c : c + 1],
                )

        def add_up(b, batch):
            if b == batch[0]:
                sums[batch] = small_bank((P, len(batch), H)) if len(batch) > 1 else next_bank((P, 1, H), use="late")
            for c in range(C):
                nc.tensor.matmul(
                    out=sums[batch][:, b - batch[0], :],
                    lhsT=expd[b // 2, c // 4][:, c % 4, b % 2, :],
                    rhs=ident[:],
                    start=(c == 0),
                    stop=(c == C - 1),
                    is_transpose=True,
                )

        def turn_back(b, ch, use="turn"):
            bank = next_bank((P, 4, H), use=use)
            for c in range(4):
                nc.tensor.transpose(bank[:, c, :], expd[b // 2, ch][:, c, b % 2, :], ident[:])
            turned[b, ch] = bank

        def invert(batch, on_scalar):
            inverse = keep.tile([P, len(batch), H], F32, name="inv_sum_%d" % batch[0])
            if on_scalar:
                nc.scalar.activation(out=inverse[:], in_=sums[batch][:], func=ACT.Ln)
                nc.scalar.activation(out=inverse[:], in_=inverse[:], func=ACT.Exp, scale=-1.0)
            else:
                nc.vector.reciprocal(out=inverse[:], in_=sums[batch][:])
            for b in batch:
                inv_sum[b] = inverse[:, b - batch[0], :]

        def divide(b, ch):
            if ch == 0:
                result[b] = work.tile([P, H, C], F32, name="result", tag="result", bufs=5)
            nc.vector.tensor_tensor(
                out=result[b][:, :, 4 * ch : 4 * ch + 4],
                in0=turned[b, ch][:].rearrange("p c h -> p h c"),
                in1=inv_sum[b].unsqueeze(2).broadcast_to([P, H, 4]),
                op=ALU.mult,
            )

        def store(b):
            nc.sync.dma_start(
                out=out[b * P : (b + 1) * P].rearrange("r h c -> r (h c)"), in_=result[b][:].rearrange("p h c -> p (h c)")
            )

        units = [(0, 0), (0, 1), (1, 0), (1, 1)]

        def covariances(k):
            for t in range(PACK):
                covariance(*units[k], t)

        def gains(k, ts, on_scalar):
            for t in ts:
                apply_gain(*units[k], t, on_scalar)

        spread_x_scale()
        group_u_on_scalar(0, 0)
        scale_x(0)
        spread_inv_q_on_tensor()
        group_u_on_scalar(1, 0)
        group_on_vector(("v", 0, 0), v_raw[0, 0])
        group_on_vector(("v", 1, 0), v_raw[1, 0])
        collect_inv_q()
        quantize_v(0)
        quantize_u(0)
        group_v_on_tensor(0, 1)
        row_constants()
        collect("v", 0, 1)
        covariances(0)
        group_v_on_tensor(1, 1)
        normalise(0, 0, 0)
        normalise(0, 0, 1)
        clamp(0, 0, 0, 2)
        normalise(0, 0, 2)
        normalise(0, 0, 3)
        group_u(0, 1)
        quantize_v(1, 0, 1)
        scale_x(1)
        clamp(0, 0, 2, 2)
        collect("v", 1, 1)
        quantize_v(1, 1, 1)
        covariances(1)
        logarithm(0, 0, 0, 2)
        logarithm(0, 0, 2, 2)
        collect("u", 0, 1)
        group_u(1, 1)
        scale_x(2)
        normalise(0, 1, 0)
        normalise(0, 1, 1)
        clamp(0, 1, 0, 2)
        normalise(0, 1, 2)
        normalise(0, 1, 3)
        clamp(0, 1, 2, 2)
        collect("u", 1, 1)
        quantize_u(1, 0, 1)
        gains(0, (0, 1, 2, 3), False)
        quantize_u(1, 1, 1)
        covariances(2)
        logarithm(0, 1, 0, 2)
        logarithm(0, 1, 2, 2)
        group_w(0, 0)
        gains(1, (0, 1), True)
        normalise(1, 0, 0)
        normalise(1, 0, 1)
        clamp(1, 0, 0, 2)
        normalise(1, 0, 2)
        normalise(1, 0, 3)
        clamp(1, 0, 2, 2)
        covariances(3)
        turn_x(0)
        turn_x(1)
        turn_x(2)
        scale_x(3)
        logarithm(1, 0, 0, 2)
        logarithm(1, 0, 2, 2)
        for t in range(PACK):
            normalise(1, 1, t)
        turn_x(3)
        gains(1, (2, 3), True)
        clamp(1, 1, 0, 2)
        clamp(1, 1, 2, 2)
        scale_x(4)
        turn_x(4)
        group_w(0, 1)
        gains(2, (0, 1), True)
        logarithm(1, 1, 0, 2)
        logarithm(1, 1, 2, 2)
        gains(2, (2, 3), False)
        quantize_w(0)
        scale_x(5)
        turn_x(5)
        group_w(1, 0)
        gains(3, (2, 3), True)
        gains(3, (0, 1), False)
        collect_x(0)
        collect_x(1)
        scale_x(6)
        turn_x(6)
        group_w(1, 1)
        for b in range(2, 6):
            collect_x(b)
        quantize_x(0)
        quantize_w(1)
        support(0, 1)
        support(0, 0)
        scale_x(7)
        collect_x(6)
        park(0)
        turn_x(7)
        support(1, 1)
        support(1, 0)
        quantize_x(1)
        collect_x(7)
        park(1)

        early, late = (0, 1, 2, 3), (4, 5)

        def ahead(b):
            support(b, 1)
            park(b)

        def turn_both(b, use="late"):
            turn_back(b, 0, use)
            turn_back(b, 1, use)

        def finish(b):
            divide(b, 0)
            divide(b, 1)
            store(b)

        max_of_pairs(0)
        ahead(2)
        ahead(3)
        quantize_x(2)
        max_of_units(0)
        ahead(4)
        support(2, 0)
        quantize_x(3)
        for d in (5, 6, 7):
            support(d, 1)
        for b in range(BLOCKS):
            last = b + 1 == BLOCKS
            on_gpsimd = True and not last
            if on_gpsimd:
                shift(b, 1, nc.gpsimd)
            if not last:
                max_of_pairs(b + 1)
            shift(b, 0, nc.vector)
            if b + 3 < BLOCKS:
                support(b + 3, 0)
            if not last:
                max_of_units(b + 1)
            if not on_gpsimd:
                shift(b, 1, nc.vector)
            if b in (1, 3):
                exponentiate(b // 2)
            if b == 1:
                for d in (5, 6, 7):
                    park(d)
            if b == 3:
                add_up(0, early)
                add_up(1, early)
            if b == 4:
                add_up(2, early)
                add_up(3, early)
                invert(early, True)
                turn_both(0, "turn")
                turn_both(1)
        exponentiate(3)
        exponentiate(2)
        turn_both(2)
        turn_back(3, 0, "late")
        divide(0, 0)
        turn_back(3, 1, "late")
        divide(0, 1)
        store(0)
        add_up(6, (6,))
        finish(1)
        add_up(7, (7,))
        finish(2)
        turn_both(6)
        finish(3)
        turn_both(7)
        add_up(4, late)
        add_up(5, late)
        invert(late, True)
        invert((6,), False)
        invert((7,), False)
        finish(6)
        turn_both(4)
        turn_both(5)
        finish(7)
        finish(4)
        finish(5)
